import numpy as np
import ml_dtypes


def mxq(x, axis, fmt="e4m3"):
    dtype, down = {"e4m3": (ml_dtypes.float8_e4m3fn, 7), "e5m2": (ml_dtypes.float8_e5m2, 14)}[fmt]
    v = np.moveaxis(np.asarray(x, np.float32).astype(ml_dtypes.bfloat16).astype(np.float64), axis, -1)
    blocks = v.reshape(v.shape[:-1] + (-1, 32))
    amax = np.abs(blocks).max(-1, keepdims=True)
    byte = np.maximum(np.where(amax > 0, np.frexp(amax)[1] - 1 + 127, 0) - down, 1)
    scale = np.exp2(byte - 127.0)
    codes = (blocks / scale).astype(np.float32).astype(dtype).astype(np.float64)
    return np.moveaxis((codes * scale).reshape(v.shape), -1, axis)


WIDE = False


def mx_kscale(k):
    if not WIDE:
        return np.ones(k)
    levels = np.array([10, -10, 5, -5, 0])
    if k % 512:
        return np.exp2(np.random.permutation(np.resize(levels, k // 32))).repeat(32)
    a = np.empty((k // 512, 16))
    for p in range(k // 512):
        a[p, :8] = np.random.permutation(np.resize(levels, 8))
        for g in range(8):
            far = levels[np.abs(levels - a[p, g]) >= 10]
            a[p, g + 8] = far[np.random.randint(len(far))]
    return np.exp2(a.ravel()).repeat(32)


def f64(x):
    return np.asarray(x).astype(np.float64)


def striped(idx):
    return np.tile(idx.reshape(-1, 16).T, (8, 1)).astype(np.uint16)


def unstriped(offs):
    return offs[:16].T.reshape(-1).astype(np.int64)


E2M1 = np.array([0.0, 0.5, 1.0, 1.5, 2.0, 3.0, 4.0, 6.0, -0.0, -0.5, -1.0, -1.5, -2.0, -3.0, -4.0, -6.0])


def pack_weight(w, fmt):
    k, n = w.shape
    w = f64(np.asarray(w, np.float32).astype(ml_dtypes.bfloat16)).reshape(k // 32, 32, n)
    amax = np.abs(w).max(1)
    if fmt == "e4m3":
        byte = np.frexp(amax)[1] - 1 + 127 - 7
    else:
        mant, ex = np.frexp(amax / 6.0)
        byte = np.where(mant > 0.5, ex, ex - 1) + 127
    byte = np.clip(np.where(amax > 0, byte, 1), 1, 254)
    scaled = (w * np.exp2(127.0 - byte)[:, None, :]).reshape(k, n).astype(np.float32)
    by_word = np.ascontiguousarray(scaled.reshape(k // 512, 128, 4, n).transpose(0, 1, 3, 2))
    if fmt == "e4m3":
        words = by_word.astype(ml_dtypes.float8_e4m3fn).view(np.uint8)
    else:
        c = by_word.astype(ml_dtypes.float4_e2m1fn).view(np.uint8) & 0xF
        words = (c[..., 0::2] | (c[..., 1::2] << 4)).reshape(k // 512, 128, 2 * n)
    return np.ascontiguousarray(words), np.ascontiguousarray(byte.astype(np.uint8).reshape(k // 512, 16, n))


def unpack_weight(words, scales, fmt):
    g, _, n = scales.shape
    words = np.ascontiguousarray(words).reshape(g, 128, n, -1)
    if fmt == "e4m3":
        vals = words.view(ml_dtypes.float8_e4m3fn).astype(np.float64)
    else:
        nib = np.empty((g, 128, n, 4), np.uint8)
        nib[..., 0::2] = words & 0xF
        nib[..., 1::2] = words >> 4
        vals = E2M1[nib]
    vals = vals * np.repeat(np.exp2(scales.astype(np.float64) - 127.0), 8, axis=1)[..., None]
    return vals.transpose(0, 1, 3, 2).reshape(g * 512, n)


def gelu(v):
    return 0.5 * v * (1.0 + np.tanh(np.sqrt(2.0 / np.pi) * (v + 0.044715 * v**3)))


def bf(x):
    return np.asarray(x, np.float32).astype(ml_dtypes.bfloat16)


def planes(Y):
    n, m = Y.shape
    b = f64(bf(Y)).reshape(n // 32, 32, m)
    amax = np.abs(b).max(1)
    byte = np.clip(np.where(amax > 0, np.frexp(amax)[1] - 1 + 127 - 7, 1), 1, 254)
    codes = (b * np.exp2(127.0 - byte)[:, None, :]).reshape(n, m).astype(np.float32).astype(ml_dtypes.float8_e4m3fn).view(np.uint8)
    words = codes.reshape(n // 512, 128, 4, m).transpose(0, 1, 3, 2)
    return np.ascontiguousarray(words), np.ascontiguousarray(byte.astype(np.uint8).reshape(n // 512, 16, m))


K, R, T, S, H, T2, P = 1024, 512, 2048, 1024, 512, 2048, 1024

def setup_inputs():
    n = np.random.standard_normal
    s, q, u = mx_kscale(K)[:, None], mx_kscale(R)[:, None], mx_kscale(H)[:, None]
    d = {}
    d["tab_words"], d["tab_scales"] = pack_weight(n((K, T)) * s, "e4m3")
    d["offs"] = striped(np.random.permutation(T)[:S])
    d["offs2"] = striped(np.random.permutation(T2)[:S])
    d["offs3"] = striped(np.random.permutation(T2)[:P])
    d["offs4"] = striped(np.random.permutation(T2)[:P])
    d["w1"] = (1.6 * n((K, R)) / K**0.5 / s).astype(np.float32)
    d["gt"] = (np.exp(0.3 * n(R)) * q[:, 0]).astype(np.float32)
    d["w2"] = (0.55 * n((R, H)) / R**0.5 / q * u.T).astype(np.float32)
    d["w3_words"], d["w3_scales"] = pack_weight(0.55 * n((R, H)) / R**0.5 / q * u.T, "e2m1")
    d["page0"] = (np.random.uniform(-1.8, 1.8, (H, T2)) * u).astype(np.float32)
    d["wgs"] = np.exp(0.3 * n((128, S))).astype(np.float32)
    d["gx"] = (np.random.uniform(1.4, 2.0, H) / u[:, 0]).astype(np.float32)
    d["ge"] = (np.exp(0.3 * n(H)) * u[:, 0]).astype(np.float32)
    d["w4_words"], d["w4_scales"] = pack_weight(n((H, H)) * np.exp(0.8 * n(H))[None, :] / H**0.5 / u, "e4m3")
    d["gg"] = (np.random.uniform(0.5, 0.62, H) / u[:, 0]).astype(np.float32)
    return d

def reference(tab_words, tab_scales, offs, offs2, offs3, offs4, w1, gt, w2, w3_words, w3_scales, page0, wgs, gx, ge, w4_words, w4_scales, gg):
    v = unpack_weight(tab_words, tab_scales, "e4m3")[:, unstriped(offs)]
    th = f64(gt)[:, None] * np.tanh(mxq(f64(w1), 0, "e4m3").T @ v)
    thq = mxq(th, 0, "e4m3")
    a = mxq(f64(w2), 0, "e4m3").T @ thq
    b = unpack_weight(w3_words, w3_scales, "e2m1").T @ thq
    h = np.minimum(a, b)
    page = f64(page0).copy()
    page[:, unstriped(offs2)] = np.tile(f64(wgs), (H // 128, 1)) * h
    x = page[:, unstriped(offs3)] * f64(gx)[:, None]
    x = 0.5 * x * (1.0 + np.tanh(0.7978845608028654 * (x + 0.044715 * x**3)))
    xq = mxq(x * f64(ge)[:, None], 0, "e4m3")
    f = unpack_weight(w4_words, w4_scales, "e4m3").T @ xq
    y = f * np.cos(page[:, unstriped(offs4)] * f64(gg)[:, None])
    words, scales = planes(y)
    return y, words, scales

@@ -1,0 +1,346 @@
+import math
+from contextlib import ExitStack
+
+import concourse.mybir as mybir
+
+F32 = mybir.dt.float32
+BF16 = mybir.dt.bfloat16
+I32 = mybir.dt.int32
+U32 = mybir.dt.uint32
+U16 = mybir.dt.uint16
+U8 = mybir.dt.uint8
+FP8X4 = mybir.dt.float8_e4m3fn_x4
+FP4X4 = mybir.dt.float4_e2m1fn_x4
+ACT = mybir.ActivationFunctionType
+ALU = mybir.AluOpType
+
+P = 128
+PACK = 4
+K, R, T, S, H, T2, NP = 1024, 512, 2048, 1024, 512, 2048, 1024
+FLOPS = 2 * K * R * S + 2 * 2 * R * H * S + 2 * H * H * NP
+HALF = 512
+S_CHUNKS = [(0, 256), (256, 256), (512, 512)]
+Y_CHUNKS = [(0, 512), (512, 256), (768, 256)]
+EARLY_GUIDES = 2
+ROUNDER = 1.5 * 2.0**23
+
+
+def tile_list_karaoke_phrase_grading_kernel(
+    tc, tab_words, tab_scales, offs, offs2, offs3, offs4, w1, gt, w2, w3_words, w3_scales,
+    page0, wgs, gx, ge, w4_words, w4_scales, gg, out_0, out_1, out_2,
+):
+    nc = tc.nc
+    with ExitStack() as ctx:
+        keep = ctx.enter_context(tc.tile_pool(name="keep", bufs=1))
+        work = ctx.enter_context(tc.tile_pool(name="work", bufs=1))
+        psum = ctx.enter_context(tc.psum_pool(name="psum", bufs=1))
+
+        def entries(lst, j0, n):
+            return lst[:, j0 // 16 : (j0 + n) // 16]
+
+        def weave(ap_tj):
+            return ap_tj.rearrange("p t (c i) -> p c t i", i=PACK)
+
+        def woven(ap_jt):
+            return ap_jt.rearrange("p (c i t) -> p c t i", i=PACK, t=PACK)
+
+        list1 = keep.tile([P, S // 16], U16, name="list1")
+        list2 = keep.tile([P, S // 16], U16, name="list2")
+        list3 = keep.tile([P, NP // 16], U16, name="list3")
+        list4 = keep.tile([P, NP // 16], U16, name="list4")
+        tab_w = [keep.tile([P, T], U32, name="tab_w%d" % a, align_bytes=64) for a in range(2)]
+        tab_s = keep.tile([P, T], U8, name="tab_s", align_bytes=64)
+        v_s = keep.tile([P, S], U8, name="v_s", align_bytes=64)
+        w3_raw = keep.tile([P, 2 * H], U8, name="w3_raw", align_bytes=64)
+        w3_c = keep.tile([P, 2 * H], U8, name="w3_c", align_bytes=64)
+        w34_raw = keep.tile([P, H], U8, name="w34_raw", align_bytes=64)
+        w34_s = keep.tile([P, H], U8, name="w34_s", align_bytes=64)
+        w4_raw = keep.tile([P, H], I32, name="w4_raw", align_bytes=64)
+        w4_c = keep.tile([P, H], I32, name="w4_c", align_bytes=64)
+        page = [keep.tile([P, T2], F32, name="page%d" % t) for t in range(PACK)]
+        wg = [[keep.tile([P, HALF], F32, name="wg%d_%d" % (t, h)) for h in range(2)] for t in range(PACK)]
+        gt_s = keep.tile([P, PACK], F32, name="gt_s")
+        gx_s = keep.tile([P, PACK], F32, name="gx_s")
+        ge_s = keep.tile([P, PACK], F32, name="ge_s")
+        gg_s = keep.tile([P, PACK], F32, name="gg_s")
+        turns = keep.tile([P, PACK], F32, name="turns")
+        warm = keep.tile([P, 1], F32, name="warm")
+        warm2 = keep.tile([P, 1], F32, name="warm2")
+
+        nc.vector.memset(tab_s[:].bitcast(I32), 0)
+        nc.vector.memset(w34_raw[:].bitcast(I32), 0)
+        nc.vector.memset(warm[:], 0.0)
+        nc.scalar.activation(out=warm2[:], in_=warm[:], func=ACT.Gelu_apprx_tanh)
+
+        def load_rows(w, a, name):
+            raw = work.tile([P, PACK, 512], F32, name=name, tag="raw", bufs=3, align_bytes=64)
+            nc.sync.dma_start(out=raw[:], in_=w[512 * a : 512 * (a + 1), :].rearrange("(p j) c -> p j c", j=PACK))
+            return raw
+
+        def load_tab(a):
+            nc.sync.dma_start(out=tab_w[a][:].bitcast(I32), in_=tab_words[a].rearrange("p n t -> p (n t)").bitcast(I32))
+
+        def load_wg(t, h):
+            rows = wgs.rearrange("(q t) j -> t q j", t=PACK)[t]
+            for quad in range(4):
+                nc.sync.dma_start(out=wg[t][h][32 * quad : 32 * quad + 32, :], in_=rows[:, HALF * h : HALF * (h + 1)])
+
+        def load_scales(engine, row0, scales):
+            for quad in range(4):
+                engine.dma_start(
+                    out=w34_raw[32 * quad + row0 : 32 * quad + row0 + 4, :].bitcast(I32),
+                    in_=scales[0, 4 * quad : 4 * quad + 4, :].bitcast(I32),
+                )
+
+        def load_vec(dst, vec):
+            nc.sync.dma_start(out=dst[:], in_=vec.rearrange("(p t) -> p t", t=PACK))
+
+        nc.sync.dma_start(list1[:], offs)
+        nc.sync.dma_start(out=w3_raw[:].bitcast(I32), in_=w3_words[0].bitcast(I32))
+        load_tab(0)
+        for quad in range(4):
+            nc.sync.dma_start(
+                out=tab_s[32 * quad : 32 * quad + 8, :].bitcast(I32),
+                in_=tab_scales[:, 4 * quad : 4 * quad + 4, :].bitcast(I32),
+            )
+        w1_raw = [load_rows(w1, 0, "w1_raw0")]
+        load_scales(nc.sync, 0, w3_scales)
+        w1_raw.append(load_rows(w1, 1, "w1_raw1"))
+        load_tab(1)
+        load_vec(gt_s, gt)
+        w2_raw = load_rows(w2, 0, "w2_raw")
+        nc.sync.dma_start(list2[:], offs2)
+        for t in range(PACK):
+            nc.sync.dma_start(out=page[t][:], in_=page0.rearrange("(p t) c -> t p c", t=PACK)[t])
+            load_wg(t, 0)
+        nc.sync.dma_start(list3[:], offs3)
+        load_vec(gx_s, gx)
+        load_vec(ge_s, ge)
+        load_vec(gg_s, gg)
+        nc.sync.dma_start(list4[:], offs4)
+        nc.sync.dma_start(out=w4_raw[:], in_=w4_words[0].rearrange("p n t -> p (n t)").bitcast(I32))
+        for t in range(PACK):
+            load_wg(t, 1)
+
+        load_scales(nc.gpsimd, 4, w4_scales)
+
+        nc.vector.tensor_copy(
+            out=w3_c[:].rearrange("p (t q b) -> p q t b", t=PACK, b=2),
+            in_=w3_raw[:].rearrange("p (q t b) -> p q t b", t=PACK, b=2),
+        )
+
+        def round_and_deal(engine_copy, grouped, raw, t0, t1):
+            engine_copy(
+                out=grouped[:].rearrange("p (t q j) -> p q j t", t=PACK, j=PACK)[:, :, :, t0:t1],
+                in_=raw[:].rearrange("p j (q t) -> p q j t", t=PACK)[:, :, :, t0:t1],
+            )
+
+        def gather_words(a, c):
+            j0, n = S_CHUNKS[c]
+            words = keep.tile([P, n], U32, name="v_w%d_%d" % (a, c), align_bytes=64)
+            nc.vector.tensor_copy(words[:], tab_w[a][:].indirect(entries(list1, j0, n)))
+            return words
+
+        w1_c = [keep.tile([P, R], U32, name="w1_c%d" % a, align_bytes=64) for a in range(2)]
+        w1_s = [keep.tile([P, R], U8, name="w1_s%d" % a, align_bytes=64) for a in range(2)]
+        w2_c = keep.tile([P, H], U32, name="w2_c", align_bytes=64)
+        w2_s = keep.tile([P, H], U8, name="w2_s", align_bytes=64)
+
+        def grouped_tile(name, width):
+            return work.tile([P, width], BF16, name=name, tag="grouped", bufs=3, align_bytes=64)
+
+        v_w = [[None] * len(S_CHUNKS) for a in range(2)]
+        for c in range(len(S_CHUNKS)):
+            v_w[0][c] = gather_words(0, c)
+        nc.vector.tensor_copy(v_s[:], tab_s[:].indirect(list1[:]))
+
+        w1_g0 = grouped_tile("w1_g0", PACK * R)
+        round_and_deal(nc.scalar.copy, w1_g0, w1_raw[0], 0, 4)
+        nc.vector.quantize_mx(out=w1_c[0][:].bitcast(FP8X4), scales=w1_s[0][:], in_=w1_g0[:])
+        w1_g1 = grouped_tile("w1_g1", PACK * R)
+        round_and_deal(nc.scalar.copy, w1_g1, w1_raw[1], 0, 2)
+        round_and_deal(nc.vector.tensor_copy, w1_g1, w1_raw[1], 2, 4)
+        nc.vector.quantize_mx(out=w1_c[1][:].bitcast(FP8X4), scales=w1_s[1][:], in_=w1_g1[:])
+        for c in range(len(S_CHUNKS)):
+            v_w[1][c] = gather_words(1, c)
+
+        th_c, th_s = {}, {}
+        th32, th_g = {}, {}
+
+        def first_product(c):
+            j0, n = S_CHUNKS[c]
+            banks = [psum.tile([P, n], F32, name="z%d_%d" % (c, t), tag="z%d" % t) for t in range(PACK)]
+            for a in range(2):
+                for t in range(PACK):
+                    cols = slice(P * t, P * (t + 1))
+                    nc.tensor.matmul_mx(
+                        out=banks[t][:],
+                        lhsT=w1_c[a][:, cols].bitcast(FP8X4), lhsT_scale=w1_s[a][:, cols],
+                        rhs=v_w[a][c][:].bitcast(FP8X4), rhs_scale=v_s[4 * a : P, j0 : j0 + n],
+                        start=(a == 0), stop=(a == 1),
+                    )
+            th32[c] = work.tile([P, PACK, n], F32, name="th32_%d" % c, tag="th32")
+            for t in range(PACK):
+                nc.scalar.activation(out=th32[c][:, t, :], in_=banks[t][:], func=ACT.Tanh)
+
+        def gain_on_vector(c):
+            j0, n = S_CHUNKS[c]
+            th_g[c] = work.tile([P, PACK * n], BF16, name="th_g%d" % c, tag="th_g", bufs=2, align_bytes=64)
+            gains = gt_s[:].rearrange("p (c t i) -> p c t i", c=1, i=1).to_broadcast([P, n // PACK, PACK, PACK])
+            nc.vector.tensor_tensor(out=woven(th_g[c][:]), in0=weave(th32[c][:]), in1=gains, op=ALU.mult)
+
+        def gain_on_scalar(c):
+            j0, n = S_CHUNKS[c]
+            th16 = work.tile([P, PACK, n], BF16, name="th16_%d" % c, tag="th16")
+            for t in range(PACK):
+                nc.scalar.activation(out=th16[:, t, :], in_=th32[c][:, t, :], func=ACT.Copy, scale=gt_s[:, t : t + 1])
+            th_g[c] = work.tile([P, PACK * n], BF16, name="th_g%d" % c, tag="th_g", bufs=2, align_bytes=64)
+            nc.scalar.copy(out=woven(th_g[c][:]), in_=weave(th16[:]))
+
+        def quantise_th(c):
+            j0, n = S_CHUNKS[c]
+            th_c[c] = keep.tile([P, n], U32, name="th_c%d" % c, align_bytes=64)
+            th_s[c] = keep.tile([P, n], U8, name="th_s%d" % c, align_bytes=64)
+            nc.vector.quantize_mx(out=th_c[c][:].bitcast(FP8X4), scales=th_s[c][:], in_=th_g[c][:])
+
+        w2_g = grouped_tile("w2_g", PACK * H)
+
+        def quantise_w2(t0, t1):
+            round_and_deal(nc.scalar.copy, w2_g, w2_raw, t0, t1)
+            cols = slice(P * t0, P * t1)
+            nc.vector.quantize_mx(
+                out=w2_c[:, cols].bitcast(FP8X4), scales=w2_s[:, cols], in_=w2_g[:, PACK * P * t0 : PACK * P * t1]
+            )
+
+        h_of = {}
+
+        def smaller_feature(c, t):
+            j0, n = S_CHUNKS[c]
+            cols = slice(P * t, P * (t + 1))
+            bank_a = psum.tile([P, n], F32, name="a%d_%d" % (c, t), tag="a", bufs=2)
+            bank_b = psum.tile([P, n], F32, name="b%d_%d" % (c, t), tag="b", bufs=2)
+            nc.tensor.matmul_mx(
+                out=bank_a[:], lhsT=w2_c[:, cols].bitcast(FP8X4), lhsT_scale=w2_s[:, cols],
+                rhs=th_c[c][:].bitcast(FP8X4), rhs_scale=th_s[c][:], start=True, stop=True,
+            )
+            nc.tensor.matmul_mx(
+                out=bank_b[:], lhsT=w3_c[:, 2 * P * t : 2 * P * (t + 1)].bitcast(FP4X4), lhsT_scale=w34_s[:, cols],
+                rhs=th_c[c][:].bitcast(FP8X4), rhs_scale=th_s[c][:], start=True, stop=True,
+            )
+            a32 = work.tile([P, n], F32, name="a32_%d_%d" % (c, t), tag="a32", bufs=2)
+            nc.scalar.copy(out=a32[:], in_=bank_a[:])
+            h_of[c, t] = work.tile([P, n], F32, name="h%d_%d" % (c, t), tag="h", bufs=3)
+            nc.vector.tensor_tensor(out=h_of[c, t][:], in0=bank_b[:], in1=a32[:], op=ALU.min)
+
+        def scatter(c, t):
+            j0, n = S_CHUNKS[c]
+            w_cols = wg[t][j0 // HALF][:, j0 % HALF : j0 % HALF + n]
+            nc.vector.tensor_tensor(page[t][:].indirect(entries(list2, j0, n)), h_of[c, t][:], w_cols, ALU.mult)
+
+        gelu32 = work.tile([P, PACK, NP], F32, name="gelu32", tag="gelu_cos")
+        x_g = [None, None]
+
+        def review(t, h):
+            if x_g[h] is None:
+                x_g[h] = grouped_tile("x_g%d" % h, PACK * HALF)
+            cols = slice(HALF * h, HALF * (h + 1))
+            picked = work.tile([P, HALF], F32, name="g3_%d_%d" % (t, h), tag="g3", bufs=2)
+            nc.vector.tensor_copy(picked[:], page[t][:].indirect(entries(list3, HALF * h, HALF)))
+            nc.scalar.activation(out=gelu32[:, t, cols], in_=picked[:], func=ACT.Gelu_apprx_tanh, scale=gx_s[:, t : t + 1])
+            nc.scalar.activation(
+                out=x_g[h][:].rearrange("p (j t) -> p t j", t=PACK)[:, t, :], in_=gelu32[:, t, cols],
+                func=ACT.Copy, scale=ge_s[:, t : t + 1],
+            )
+
+        u_of, k_of = {}, {}
+        rest = work.tile([P, PACK, NP], F32, name="rest")
+
+        def guide(t, h):
+            picked = work.tile([P, HALF], F32, name="g4_%d_%d" % (t, h), tag="g4", bufs=3)
+            nc.vector.tensor_copy(picked[:], page[t][:].indirect(entries(list4, HALF * h, HALF)))
+            u_of[t, h] = work.tile([P, HALF], F32, name="u%d_%d" % (t, h), tag="u", bufs=3)
+            k_of[t, h] = work.tile([P, HALF], U32, name="k%d_%d" % (t, h), tag="k", bufs=3)
+            nc.scalar.activation(out=u_of[t, h][:], in_=picked[:], func=ACT.Copy, scale=turns[:, t : t + 1], bias=0.25)
+            nc.scalar.activation(out=k_of[t, h][:], in_=u_of[t, h][:], func=ACT.Copy, bias=ROUNDER)
+
+        def reduce_turns(t, h):
+            nc.vector.scalar_tensor_tensor(
+                out=rest[:, t, HALF * h : HALF * (h + 1)], in0=k_of[t, h][:].bitcast(I32), scalar=ROUNDER,
+                in1=u_of[t, h][:], op0=ALU.subtract, op1=ALU.subtract,
+            )
+
+        first_product(0)
+        nc.vector.tensor_copy(
+            out=w34_s[:].rearrange("p (t q) -> p q t", t=PACK), in_=w34_raw[:].rearrange("p (q t) -> p q t", t=PACK)
+        )
+        gain_on_vector(0)
+        quantise_w2(0, 2)
+        quantise_th(0)
+        smaller_feature(0, 0)
+        quantise_w2(2, 4)
+        nc.gpsimd.tensor_scalar(
+            out=turns[:], in0=gg_s[:], scalar1=1.0 / (2.0 * math.pi), scalar2=0.0, op0=ALU.mult, op1=ALU.add
+        )
+
+        last = len(S_CHUNKS) - 1
+        units = [(c, t) for c in range(len(S_CHUNKS)) for t in range(PACK)]
+        for i, (c, t) in enumerate(units):
+            if c < last and t == 0:
+                first_product(c + 1)
+            if c < last and t == 1:
+                gain_on_scalar(c + 1)
+            if c < last and t == 2:
+                quantise_th(c + 1)
+            if i + 1 < len(units):
+                smaller_feature(*units[i + 1])
+            scatter(c, t)
+            if c == last:
+                early = 0 < t <= EARLY_GUIDES
+                if early:
+                    guide(t - 1, 0)
+                review(t, 0)
+                review(t, 1)
+                if early:
+                    guide(t - 1, 1)
+                    reduce_turns(t - 1, 0)
+                    reduce_turns(t - 1, 1)
+            if (c, t) == (0, 3):
+                nc.vector.tensor_copy(
+                    out=w4_c[:].rearrange("p (t q) -> p q t", t=PACK), in_=w4_raw[:].rearrange("p (q t) -> p q t", t=PACK)
+                )
+
+        x_c = [keep.tile([P, HALF], U32, name="x_c%d" % h, align_bytes=64) for h in range(2)]
+        x_s = [keep.tile([P, HALF], U8, name="x_s%d" % h, align_bytes=64) for h in range(2)]
+        cos32 = work.tile([P, PACK, NP], F32, name="cos32", tag="gelu_cos")
+        for h in range(2):
+            for t in range(EARLY_GUIDES, PACK):
+                guide(t, h)
+            nc.vector.quantize_mx(out=x_c[h][:].bitcast(FP8X4), scales=x_s[h][:], in_=x_g[h][:])
+            for t in range(EARLY_GUIDES, PACK):
+                reduce_turns(t, h)
+
+        y_s = keep.tile([P, NP], U8, name="y_s", align_bytes=64)
+        out_rows = out_0.rearrange("(p t) j -> p t j", t=PACK)
+        out_words = out_1[0].rearrange("p n t -> p (n t)").bitcast(I32)
+        for c, (j0, n) in enumerate(Y_CHUNKS):
+            h, cols, xc = j0 // HALF, slice(j0, j0 + n), slice(j0 % HALF, j0 % HALF + n)
+            y32 = work.tile([P, PACK, n], F32, name="y32_%d" % c, tag="raw", bufs=3, align_bytes=64)
+            for t in range(PACK):
+                wc = slice(P * t, P * (t + 1))
+                bank = psum.tile([P, n], F32, name="f%d_%d" % (c, t), tag="z%d" % t)
+                nc.tensor.matmul_mx(
+                    out=bank[:], lhsT=w4_c[:, wc].bitcast(FP8X4), lhsT_scale=w34_s[4:P, wc],
+                    rhs=x_c[h][:, xc].bitcast(FP8X4), rhs_scale=x_s[h][:, xc], start=True, stop=True,
+                )
+                nc.scalar.activation(out=cos32[:, t, cols], in_=rest[:, t, cols], func=ACT.Sin, scale=-2.0 * math.pi)
+                nc.vector.tensor_tensor(out=y32[:, t, :], in0=bank[:], in1=cos32[:, t, cols], op=ALU.mult)
+            nc.sync.dma_start(out=out_rows[:, :, cols], in_=y32[:])
+            y_g = grouped_tile("y_g%d" % c, PACK * n)
+            nc.scalar.copy(out=woven(y_g[:]), in_=weave(y32[:]))
+            y_c = keep.tile([P, n], U32, name="y_c%d" % c, align_bytes=64)
+            nc.vector.quantize_mx(out=y_c[:].bitcast(FP8X4), scales=y_s[:, cols], in_=y_g[:])
+            nc.sync.dma_start(out=out_words[:, cols], in_=y_c[:].bitcast(I32))
+        for quad in range(4):
+            nc.sync.dma_start(
+                out=out_2[0, 4 * quad : 4 * quad + 4, :].bitcast(I32), in_=y_s[32 * quad : 32 * quad + 4, :].bitcast(I32)
+            )

@@ -21,7 +21,6 @@ FLOPS = 2 * K * R * S + 2 * 2 * R * H * S + 2 * H * H * NP
 HALF = 512
 S_CHUNKS = [(0, 256), (256, 256), (512, 512)]
 Y_CHUNKS = [(0, 512), (512, 256), (768, 256)]
-EARLY_GUIDES = 2
 ROUNDER = 1.5 * 2.0**23
 
 
@@ -50,15 +49,13 @@ def tile_list_karaoke_phrase_grading_kernel(
         list4 = keep.tile([P, NP // 16], U16, name="list4")
         tab_w = [keep.tile([P, T], U32, name="tab_w%d" % a, align_bytes=64) for a in range(2)]
         tab_s = keep.tile([P, T], U8, name="tab_s", align_bytes=64)
-        v_s = keep.tile([P, S], U8, name="v_s", align_bytes=64)
         w3_raw = keep.tile([P, 2 * H], U8, name="w3_raw", align_bytes=64)
         w3_c = keep.tile([P, 2 * H], U8, name="w3_c", align_bytes=64)
         w34_raw = keep.tile([P, H], U8, name="w34_raw", align_bytes=64)
         w34_s = keep.tile([P, H], U8, name="w34_s", align_bytes=64)
         w4_raw = keep.tile([P, H], I32, name="w4_raw", align_bytes=64)
-        w4_c = keep.tile([P, H], I32, name="w4_c", align_bytes=64)
         page = [keep.tile([P, T2], F32, name="page%d" % t) for t in range(PACK)]
-        wg = [[keep.tile([P, HALF], F32, name="wg%d_%d" % (t, h)) for h in range(2)] for t in range(PACK)]
+        wg = [keep.tile([P, PACK, n], F32, name="wg%d" % c) for c, (j0, n) in enumerate(S_CHUNKS)]
         gt_s = keep.tile([P, PACK], F32, name="gt_s")
         gx_s = keep.tile([P, PACK], F32, name="gx_s")
         ge_s = keep.tile([P, PACK], F32, name="ge_s")
@@ -67,8 +64,8 @@ def tile_list_karaoke_phrase_grading_kernel(
         warm = keep.tile([P, 1], F32, name="warm")
         warm2 = keep.tile([P, 1], F32, name="warm2")
 
-        nc.vector.memset(tab_s[:].bitcast(I32), 0)
-        nc.vector.memset(w34_raw[:].bitcast(I32), 0)
+        nc.gpsimd.memset(w34_raw[:].bitcast(I32), 0)
+        nc.gpsimd.memset(tab_s[:].bitcast(I32), 0)
         nc.vector.memset(warm[:], 0.0)
         nc.scalar.activation(out=warm2[:], in_=warm[:], func=ACT.Gelu_apprx_tanh)
 
@@ -80,10 +77,14 @@ def tile_list_karaoke_phrase_grading_kernel(
         def load_tab(a):
             nc.sync.dma_start(out=tab_w[a][:].bitcast(I32), in_=tab_words[a].rearrange("p n t -> p (n t)").bitcast(I32))
 
-        def load_wg(t, h):
-            rows = wgs.rearrange("(q t) j -> t q j", t=PACK)[t]
+        def load_wg(c):
+            j0, n = S_CHUNKS[c]
+            rows = wgs.rearrange("(q t) j -> q t j", t=PACK)[:, :, j0 : j0 + n]
             for quad in range(4):
-                nc.sync.dma_start(out=wg[t][h][32 * quad : 32 * quad + 32, :], in_=rows[:, HALF * h : HALF * (h + 1)])
+                nc.sync.dma_start(out=wg[c][32 * quad : 32 * quad + 32, :, :], in_=rows)
+
+        def load_page(t):
+            nc.sync.dma_start(out=page[t][:], in_=page0.rearrange("(p t) c -> t p c", t=PACK)[t])
 
         def load_scales(engine, row0, scales):
             for quad in range(4):
@@ -107,22 +108,23 @@ def tile_list_karaoke_phrase_grading_kernel(
         load_scales(nc.sync, 0, w3_scales)
         w1_raw.append(load_rows(w1, 1, "w1_raw1"))
         load_tab(1)
-        load_vec(gt_s, gt)
+        load_scales(nc.sync, 4, w4_scales)
         w2_raw = load_rows(w2, 0, "w2_raw")
+        load_vec(gt_s, gt)
+        load_vec(gg_s, gg)
         nc.sync.dma_start(list2[:], offs2)
-        for t in range(PACK):
-            nc.sync.dma_start(out=page[t][:], in_=page0.rearrange("(p t) c -> t p c", t=PACK)[t])
-            load_wg(t, 0)
+        load_page(0)
+        load_wg(0)
+        for t in range(1, PACK):
+            load_page(t)
+        load_wg(1)
         nc.sync.dma_start(list3[:], offs3)
         load_vec(gx_s, gx)
         load_vec(ge_s, ge)
-        load_vec(gg_s, gg)
+        load_wg(2)
         nc.sync.dma_start(list4[:], offs4)
         nc.sync.dma_start(out=w4_raw[:], in_=w4_words[0].rearrange("p n t -> p (n t)").bitcast(I32))
-        for t in range(PACK):
-            load_wg(t, 1)
 
-        load_scales(nc.gpsimd, 4, w4_scales)
 
         nc.vector.tensor_copy(
             out=w3_c[:].rearrange("p (t q b) -> p q t b", t=PACK, b=2),
@@ -135,11 +137,10 @@ def tile_list_karaoke_phrase_grading_kernel(
                 in_=raw[:].rearrange("p j (q t) -> p q j t", t=PACK)[:, :, :, t0:t1],
             )
 
-        def gather_words(a, c):
+        def gather_words(words, a, c):
             j0, n = S_CHUNKS[c]
-            words = keep.tile([P, n], U32, name="v_w%d_%d" % (a, c), align_bytes=64)
-            nc.vector.tensor_copy(words[:], tab_w[a][:].indirect(entries(list1, j0, n)))
-            return words
+            v_w[a, c] = words[:, j0 : j0 + n]
+            nc.vector.tensor_copy(v_w[a, c], tab_w[a][:].indirect(entries(list1, j0, n)))
 
         w1_c = [keep.tile([P, R], U32, name="w1_c%d" % a, align_bytes=64) for a in range(2)]
         w1_s = [keep.tile([P, R], U8, name="w1_s%d" % a, align_bytes=64) for a in range(2)]
@@ -149,23 +150,30 @@ def tile_list_karaoke_phrase_grading_kernel(
         def grouped_tile(name, width):
             return work.tile([P, width], BF16, name=name, tag="grouped", bufs=3, align_bytes=64)
 
-        v_w = [[None] * len(S_CHUNKS) for a in range(2)]
-        for c in range(len(S_CHUNKS)):
-            v_w[0][c] = gather_words(0, c)
-        nc.vector.tensor_copy(v_s[:], tab_s[:].indirect(list1[:]))
+        v_w, v_s = {}, {}
 
+        def gather_scales(c):
+            j0, n = S_CHUNKS[c]
+            v_s[c] = keep.tile([P, n], U8, name="v_s%d" % c, align_bytes=64)
+            nc.vector.tensor_copy(v_s[c][:], tab_s[:].indirect(entries(list1, j0, n)))
+
+        v_w0 = keep.tile([P, S], U32, name="v_w0", align_bytes=64)
+        for c in range(len(S_CHUNKS)):
+            gather_words(v_w0, 0, c)
+            gather_scales(c)
         w1_g0 = grouped_tile("w1_g0", PACK * R)
         round_and_deal(nc.scalar.copy, w1_g0, w1_raw[0], 0, 4)
-        nc.vector.quantize_mx(out=w1_c[0][:].bitcast(FP8X4), scales=w1_s[0][:], in_=w1_g0[:])
-        w1_g1 = grouped_tile("w1_g1", PACK * R)
+        w1_g1 = work.tile([P, PACK * R], BF16, name="w1_g1", tag="second_pass", align_bytes=64)
         round_and_deal(nc.scalar.copy, w1_g1, w1_raw[1], 0, 2)
         round_and_deal(nc.vector.tensor_copy, w1_g1, w1_raw[1], 2, 4)
-        nc.vector.quantize_mx(out=w1_c[1][:].bitcast(FP8X4), scales=w1_s[1][:], in_=w1_g1[:])
+        for a, w1_g in enumerate((w1_g0, w1_g1)):
+            nc.vector.quantize_mx(out=w1_c[a][:].bitcast(FP8X4), scales=w1_s[a][:], in_=w1_g[:])
+        v_w1 = work.tile([P, S], U32, name="v_w1", tag="second_pass", align_bytes=64)
         for c in range(len(S_CHUNKS)):
-            v_w[1][c] = gather_words(1, c)
+            gather_words(v_w1, 1, c)
 
         th_c, th_s = {}, {}
-        th32, th_g = {}, {}
+        th32, th16, th_g = {}, {}, {}
 
         def first_product(c):
             j0, n = S_CHUNKS[c]
@@ -176,7 +184,7 @@ def tile_list_karaoke_phrase_grading_kernel(
                     nc.tensor.matmul_mx(
                         out=banks[t][:],
                         lhsT=w1_c[a][:, cols].bitcast(FP8X4), lhsT_scale=w1_s[a][:, cols],
-                        rhs=v_w[a][c][:].bitcast(FP8X4), rhs_scale=v_s[4 * a : P, j0 : j0 + n],
+                        rhs=v_w[a, c].bitcast(FP8X4), rhs_scale=v_s[c][4 * a : P, :],
                         start=(a == 0), stop=(a == 1),
                     )
             th32[c] = work.tile([P, PACK, n], F32, name="th32_%d" % c, tag="th32")
@@ -191,11 +199,14 @@ def tile_list_karaoke_phrase_grading_kernel(
 
         def gain_on_scalar(c):
             j0, n = S_CHUNKS[c]
-            th16 = work.tile([P, PACK, n], BF16, name="th16_%d" % c, tag="th16")
+            th16[c] = work.tile([P, PACK, n], BF16, name="th16_%d" % c, tag="th16", align_bytes=64)
             for t in range(PACK):
-                nc.scalar.activation(out=th16[:, t, :], in_=th32[c][:, t, :], func=ACT.Copy, scale=gt_s[:, t : t + 1])
+                nc.scalar.activation(out=th16[c][:, t, :], in_=th32[c][:, t, :], func=ACT.Copy, scale=gt_s[:, t : t + 1])
+
+        def weave_th(c):
+            j0, n = S_CHUNKS[c]
             th_g[c] = work.tile([P, PACK * n], BF16, name="th_g%d" % c, tag="th_g", bufs=2, align_bytes=64)
-            nc.scalar.copy(out=woven(th_g[c][:]), in_=weave(th16[:]))
+            nc.scalar.copy(out=woven(th_g[c][:]), in_=weave(th16[c][:]))
 
         def quantise_th(c):
             j0, n = S_CHUNKS[c]
@@ -205,14 +216,16 @@ def tile_list_karaoke_phrase_grading_kernel(
 
         w2_g = grouped_tile("w2_g", PACK * H)
 
-        def quantise_w2(t0, t1):
-            round_and_deal(nc.scalar.copy, w2_g, w2_raw, t0, t1)
+        def quantise_w2(engine_copy, t0, t1):
+            round_and_deal(engine_copy, w2_g, w2_raw, t0, t1)
             cols = slice(P * t0, P * t1)
             nc.vector.quantize_mx(
                 out=w2_c[:, cols].bitcast(FP8X4), scales=w2_s[:, cols], in_=w2_g[:, PACK * P * t0 : PACK * P * t1]
             )
 
         h_of = {}
+        last = len(S_CHUNKS) - 1
+        stage = [keep.tile([P, HALF], F32, name="stage%d" % i) for i in range(PACK)]
 
         def smaller_feature(c, t):
             j0, n = S_CHUNKS[c]
@@ -227,28 +240,31 @@ def tile_list_karaoke_phrase_grading_kernel(
                 out=bank_b[:], lhsT=w3_c[:, 2 * P * t : 2 * P * (t + 1)].bitcast(FP4X4), lhsT_scale=w34_s[:, cols],
                 rhs=th_c[c][:].bitcast(FP8X4), rhs_scale=th_s[c][:], start=True, stop=True,
             )
-            a32 = work.tile([P, n], F32, name="a32_%d_%d" % (c, t), tag="a32", bufs=2)
+            if c < last:
+                a32 = work.tile([P, n], F32, name="a32_%d_%d" % (c, t), tag="a32", bufs=2)
+                h_of[c, t] = work.tile([P, n], F32, name="h%d_%d" % (c, t), tag="h", bufs=2)
+            else:
+                a32, h_of[c, t] = stage[2], stage[0]
             nc.scalar.copy(out=a32[:], in_=bank_a[:])
-            h_of[c, t] = work.tile([P, n], F32, name="h%d_%d" % (c, t), tag="h", bufs=3)
             nc.vector.tensor_tensor(out=h_of[c, t][:], in0=bank_b[:], in1=a32[:], op=ALU.min)
 
         def scatter(c, t):
             j0, n = S_CHUNKS[c]
-            w_cols = wg[t][j0 // HALF][:, j0 % HALF : j0 % HALF + n]
-            nc.vector.tensor_tensor(page[t][:].indirect(entries(list2, j0, n)), h_of[c, t][:], w_cols, ALU.mult)
+            nc.vector.tensor_tensor(page[t][:].indirect(entries(list2, j0, n)), h_of[c, t][:], wg[c][:, t, :], ALU.mult)
 
-        gelu32 = work.tile([P, PACK, NP], F32, name="gelu32", tag="gelu_cos")
+        gelu32 = work.tile([P, PACK, NP], F32, name="gelu32")
         x_g = [None, None]
 
         def review(t, h):
+            cols = slice(HALF * h, HALF * (h + 1))
+            nc.vector.tensor_copy(stage[h][:], page[t][:].indirect(entries(list3, HALF * h, HALF)))
+            nc.scalar.activation(out=gelu32[:, t, cols], in_=stage[h][:], func=ACT.Gelu_apprx_tanh, scale=gx_s[:, t : t + 1])
+
+        def review_gain(t, h):
             if x_g[h] is None:
                 x_g[h] = grouped_tile("x_g%d" % h, PACK * HALF)
-            cols = slice(HALF * h, HALF * (h + 1))
-            picked = work.tile([P, HALF], F32, name="g3_%d_%d" % (t, h), tag="g3", bufs=2)
-            nc.vector.tensor_copy(picked[:], page[t][:].indirect(entries(list3, HALF * h, HALF)))
-            nc.scalar.activation(out=gelu32[:, t, cols], in_=picked[:], func=ACT.Gelu_apprx_tanh, scale=gx_s[:, t : t + 1])
             nc.scalar.activation(
-                out=x_g[h][:].rearrange("p (j t) -> p t j", t=PACK)[:, t, :], in_=gelu32[:, t, cols],
+                out=x_g[h][:].rearrange("p (j t) -> p t j", t=PACK)[:, t, :], in_=gelu32[:, t, HALF * h : HALF * (h + 1)],
                 func=ACT.Copy, scale=ge_s[:, t : t + 1],
             )
 
@@ -256,11 +272,14 @@ def tile_list_karaoke_phrase_grading_kernel(
         rest = work.tile([P, PACK, NP], F32, name="rest")
 
         def guide(t, h):
-            picked = work.tile([P, HALF], F32, name="g4_%d_%d" % (t, h), tag="g4", bufs=3)
-            nc.vector.tensor_copy(picked[:], page[t][:].indirect(entries(list4, HALF * h, HALF)))
-            u_of[t, h] = work.tile([P, HALF], F32, name="u%d_%d" % (t, h), tag="u", bufs=3)
-            k_of[t, h] = work.tile([P, HALF], U32, name="k%d_%d" % (t, h), tag="k", bufs=3)
-            nc.scalar.activation(out=u_of[t, h][:], in_=picked[:], func=ACT.Copy, scale=turns[:, t : t + 1], bias=0.25)
+            nc.vector.tensor_copy(stage[(2, 0, 1, 3)[t]][:], page[t][:].indirect(entries(list4, HALF * h, HALF)))
+
+        def count_turns(t, h):
+            u_of[t, h] = work.tile([P, HALF], F32, name="u%d_%d" % (t, h), tag="u", bufs=4)
+            k_of[t, h] = work.tile([P, HALF], U32, name="k%d_%d" % (t, h), tag="k", bufs=4)
+            nc.scalar.activation(
+                out=u_of[t, h][:], in_=stage[(2, 0, 1, 3)[t]][:], func=ACT.Copy, scale=turns[:, t : t + 1], bias=0.25
+            )
             nc.scalar.activation(out=k_of[t, h][:], in_=u_of[t, h][:], func=ACT.Copy, bias=ROUNDER)
 
         def reduce_turns(t, h):
@@ -274,57 +293,52 @@ def tile_list_karaoke_phrase_grading_kernel(
             out=w34_s[:].rearrange("p (t q) -> p q t", t=PACK), in_=w34_raw[:].rearrange("p (q t) -> p q t", t=PACK)
         )
         gain_on_vector(0)
-        quantise_w2(0, 2)
+        quantise_w2(nc.scalar.copy, 0, 2)
         quantise_th(0)
         smaller_feature(0, 0)
-        quantise_w2(2, 4)
-        nc.gpsimd.tensor_scalar(
-            out=turns[:], in0=gg_s[:], scalar1=1.0 / (2.0 * math.pi), scalar2=0.0, op0=ALU.mult, op1=ALU.add
-        )
+        quantise_w2(nc.scalar.copy, 2, 4)
 
-        last = len(S_CHUNKS) - 1
-        units = [(c, t) for c in range(len(S_CHUNKS)) for t in range(PACK)]
-        for i, (c, t) in enumerate(units):
-            if c < last and t == 0:
-                first_product(c + 1)
-            if c < last and t == 1:
-                gain_on_scalar(c + 1)
-            if c < last and t == 2:
-                quantise_th(c + 1)
-            if i + 1 < len(units):
-                smaller_feature(*units[i + 1])
-            scatter(c, t)
-            if c == last:
-                early = 0 < t <= EARLY_GUIDES
-                if early:
-                    guide(t - 1, 0)
-                review(t, 0)
-                review(t, 1)
-                if early:
-                    guide(t - 1, 1)
-                    reduce_turns(t - 1, 0)
-                    reduce_turns(t - 1, 1)
-            if (c, t) == (0, 3):
+        for c in range(len(S_CHUNKS)):
+            for t in range(PACK):
+                if (c, t) != (0, 0):
+                    smaller_feature(c, t)
+                scatter(c, t)
+                if c < last and t == 0:
+                    first_product(c + 1)
+                if c < last and t == 1:
+                    gain_on_scalar(c + 1)
+                if c < last and t == 2:
+                    weave_th(c + 1)
+                    quantise_th(c + 1)
+                if c == last:
+                    review(t, 0)
+                    review(t, 1)
+                    review_gain(t, 0)
+                    if t < PACK - 1:
+                        review_gain(t, 1)
+            if c == 1:
+                w4_c = work.tile([P, H], I32, name="w4_c", tag="th16", align_bytes=64)
                 nc.vector.tensor_copy(
                     out=w4_c[:].rearrange("p (t q) -> p q t", t=PACK), in_=w4_raw[:].rearrange("p (q t) -> p q t", t=PACK)
                 )
+                nc.scalar.activation(out=turns[:], in_=gg_s[:], func=ACT.Copy, scale=1.0 / (2.0 * math.pi))
 
         x_c = [keep.tile([P, HALF], U32, name="x_c%d" % h, align_bytes=64) for h in range(2)]
         x_s = [keep.tile([P, HALF], U8, name="x_s%d" % h, align_bytes=64) for h in range(2)]
-        cos32 = work.tile([P, PACK, NP], F32, name="cos32", tag="gelu_cos")
-        for h in range(2):
-            for t in range(EARLY_GUIDES, PACK):
-                guide(t, h)
+
+        def quantise_x(h):
             nc.vector.quantize_mx(out=x_c[h][:].bitcast(FP8X4), scales=x_s[h][:], in_=x_g[h][:])
-            for t in range(EARLY_GUIDES, PACK):
-                reduce_turns(t, h)
 
         y_s = keep.tile([P, NP], U8, name="y_s", align_bytes=64)
         out_rows = out_0.rearrange("(p t) j -> p t j", t=PACK)
         out_words = out_1[0].rearrange("p n t -> p (n t)").bitcast(I32)
-        for c, (j0, n) in enumerate(Y_CHUNKS):
+        cos32 = gelu32
+        y32 = {}
+
+        def modulate(c):
+            j0, n = Y_CHUNKS[c]
             h, cols, xc = j0 // HALF, slice(j0, j0 + n), slice(j0 % HALF, j0 % HALF + n)
-            y32 = work.tile([P, PACK, n], F32, name="y32_%d" % c, tag="raw", bufs=3, align_bytes=64)
+            y32[c] = work.tile([P, PACK, n], F32, name="y32_%d" % c, tag="raw", bufs=3, align_bytes=64)
             for t in range(PACK):
                 wc = slice(P * t, P * (t + 1))
                 bank = psum.tile([P, n], F32, name="f%d_%d" % (c, t), tag="z%d" % t)
@@ -333,13 +347,36 @@ def tile_list_karaoke_phrase_grading_kernel(
                     rhs=x_c[h][:, xc].bitcast(FP8X4), rhs_scale=x_s[h][:, xc], start=True, stop=True,
                 )
                 nc.scalar.activation(out=cos32[:, t, cols], in_=rest[:, t, cols], func=ACT.Sin, scale=-2.0 * math.pi)
-                nc.vector.tensor_tensor(out=y32[:, t, :], in0=bank[:], in1=cos32[:, t, cols], op=ALU.mult)
-            nc.sync.dma_start(out=out_rows[:, :, cols], in_=y32[:])
+                nc.vector.tensor_tensor(out=y32[c][:, t, :], in0=bank[:], in1=cos32[:, t, cols], op=ALU.mult)
+            nc.sync.dma_start(out=out_rows[:, :, cols], in_=y32[c][:])
+
+        def planes(c, engine_copy):
+            j0, n = Y_CHUNKS[c]
+            cols = slice(j0, j0 + n)
             y_g = grouped_tile("y_g%d" % c, PACK * n)
-            nc.scalar.copy(out=woven(y_g[:]), in_=weave(y32[:]))
+            engine_copy(out=woven(y_g[:]), in_=weave(y32[c][:]))
             y_c = keep.tile([P, n], U32, name="y_c%d" % c, align_bytes=64)
             nc.vector.quantize_mx(out=y_c[:].bitcast(FP8X4), scales=y_s[:, cols], in_=y_g[:])
             nc.sync.dma_start(out=out_words[:, cols], in_=y_c[:].bitcast(I32))
+
+        for t in range(PACK):
+            guide(t, 0)
+            count_turns(t, 0)
+        quantise_x(0)
+        for t in range(PACK):
+            reduce_turns(t, 0)
+            guide(t, 1)
+        review_gain(PACK - 1, 1)
+        quantise_x(1)
+        modulate(0)
+        for t in range(PACK):
+            count_turns(t, 1)
+            reduce_turns(t, 1)
+        planes(0, nc.scalar.copy)
+        modulate(1)
+        modulate(2)
+        planes(1, nc.scalar.copy)
+        planes(2, nc.vector.tensor_copy)
         for quad in range(4):
             nc.sync.dma_start(
                 out=out_2[0, 4 * quad : 4 * quad + 4, :].bitcast(I32), in_=y_s[32 * quad : 32 * quad + 4, :].bitcast(I32)

@@ -19,6 +19,7 @@ PACK = 4
 K, R, T, S, H, T2, NP = 1024, 512, 2048, 1024, 512, 2048, 1024
 FLOPS = 2 * K * R * S + 2 * 2 * R * H * S + 2 * H * H * NP
 HALF = 512
+BANK = 512
 S_CHUNKS = [(0, 256), (256, 256), (512, 512)]
 Y_CHUNKS = [(0, 512), (512, 256), (768, 256)]
 ROUNDER = 1.5 * 2.0**23
@@ -55,7 +56,6 @@ def tile_list_karaoke_phrase_grading_kernel(
         w34_s = keep.tile([P, H], U8, name="w34_s", align_bytes=64)
         w4_raw = keep.tile([P, H], I32, name="w4_raw", align_bytes=64)
         page = [keep.tile([P, T2], F32, name="page%d" % t) for t in range(PACK)]
-        wg = [keep.tile([P, PACK, n], F32, name="wg%d" % c) for c, (j0, n) in enumerate(S_CHUNKS)]
         gt_s = keep.tile([P, PACK], F32, name="gt_s")
         gx_s = keep.tile([P, PACK], F32, name="gx_s")
         ge_s = keep.tile([P, PACK], F32, name="ge_s")
@@ -77,11 +77,16 @@ def tile_list_karaoke_phrase_grading_kernel(
         def load_tab(a):
             nc.sync.dma_start(out=tab_w[a][:].bitcast(I32), in_=tab_words[a].rearrange("p n t -> p (n t)").bitcast(I32))
 
-        def load_wg(c):
+        wg = {}
+
+        def load_wg(c, t0, t1):
             j0, n = S_CHUNKS[c]
-            rows = wgs.rearrange("(q t) j -> q t j", t=PACK)[:, :, j0 : j0 + n]
+            tile = work.tile([P, t1 - t0, n], F32, name="wg%d_%d" % (c, t0), tag="wg%d_%d" % (c, t0), align_bytes=64)
+            rows = wgs.rearrange("(q t) j -> q t j", t=PACK)[:, t0:t1, j0 : j0 + n]
             for quad in range(4):
-                nc.sync.dma_start(out=wg[c][32 * quad : 32 * quad + 32, :, :], in_=rows)
+                nc.sync.dma_start(out=tile[32 * quad : 32 * quad + 32, :, :], in_=rows)
+            for t in range(t0, t1):
+                wg[c, t] = tile[:, t - t0, :]
 
         def load_page(t):
             nc.sync.dma_start(out=page[t][:], in_=page0.rearrange("(p t) c -> t p c", t=PACK)[t])
@@ -114,14 +119,17 @@ def tile_list_karaoke_phrase_grading_kernel(
         load_vec(gg_s, gg)
         nc.sync.dma_start(list2[:], offs2)
         load_page(0)
-        load_wg(0)
-        for t in range(1, PACK):
-            load_page(t)
-        load_wg(1)
+        load_wg(0, 0, 2)
+        load_page(1)
+        load_page(2)
+        load_wg(0, 2, 4)
+        load_page(3)
+        load_wg(1, 0, 2)
+        load_wg(1, 2, 4)
         nc.sync.dma_start(list3[:], offs3)
         load_vec(gx_s, gx)
         load_vec(ge_s, ge)
-        load_wg(2)
+        load_wg(2, 0, 4)
         nc.sync.dma_start(list4[:], offs4)
         nc.sync.dma_start(out=w4_raw[:], in_=w4_words[0].rearrange("p n t -> p (n t)").bitcast(I32))
 
@@ -210,7 +218,8 @@ def tile_list_karaoke_phrase_grading_kernel(
 
         def quantise_th(c):
             j0, n = S_CHUNKS[c]
-            th_c[c] = keep.tile([P, n], U32, name="th_c%d" % c, align_bytes=64)
+            place = "wg%d_0" % (c - 1) if c > 0 else "th_c0"
+            th_c[c] = work.tile([P, n], U32, name="th_c%d" % c, tag=place, align_bytes=64)
             th_s[c] = keep.tile([P, n], U8, name="th_s%d" % c, align_bytes=64)
             nc.vector.quantize_mx(out=th_c[c][:].bitcast(FP8X4), scales=th_s[c][:], in_=th_g[c][:])
 
@@ -223,42 +232,61 @@ def tile_list_karaoke_phrase_grading_kernel(
                 out=w2_c[:, cols].bitcast(FP8X4), scales=w2_s[:, cols], in_=w2_g[:, PACK * P * t0 : PACK * P * t1]
             )
 
-        h_of = {}
         last = len(S_CHUNKS) - 1
-        stage = [keep.tile([P, HALF], F32, name="stage%d" % i) for i in range(PACK)]
+        units = []
+        for c, (j0, n) in enumerate(S_CHUNKS):
+            per_bank = BANK // n
+            units.extend((c, t0, t0 + per_bank) for t0 in range(0, PACK, per_bank))
+        a_of, b_of = {}, {}
+        h32 = keep.tile([P, BANK], F32, name="h32")
 
-        def smaller_feature(c, t):
-            j0, n = S_CHUNKS[c]
-            cols = slice(P * t, P * (t + 1))
-            bank_a = psum.tile([P, n], F32, name="a%d_%d" % (c, t), tag="a", bufs=2)
-            bank_b = psum.tile([P, n], F32, name="b%d_%d" % (c, t), tag="b", bufs=2)
-            nc.tensor.matmul_mx(
-                out=bank_a[:], lhsT=w2_c[:, cols].bitcast(FP8X4), lhsT_scale=w2_s[:, cols],
-                rhs=th_c[c][:].bitcast(FP8X4), rhs_scale=th_s[c][:], start=True, stop=True,
-            )
-            nc.tensor.matmul_mx(
-                out=bank_b[:], lhsT=w3_c[:, 2 * P * t : 2 * P * (t + 1)].bitcast(FP4X4), lhsT_scale=w34_s[:, cols],
-                rhs=th_c[c][:].bitcast(FP8X4), rhs_scale=th_s[c][:], start=True, stop=True,
-            )
-            if c < last:
-                a32 = work.tile([P, n], F32, name="a32_%d_%d" % (c, t), tag="a32", bufs=2)
-                h_of[c, t] = work.tile([P, n], F32, name="h%d_%d" % (c, t), tag="h", bufs=2)
+        def second_products(i):
+            c, t0, t1 = units[i]
+            n = S_CHUNKS[c][1]
+            bank_a = psum.tile([P, BANK], F32, name="a%d" % i, tag="a", bufs=2)
+            b_of[i] = psum.tile([P, BANK], F32, name="b%d" % i, tag="b", bufs=2)
+            for t in range(t0, t1):
+                cols, out_cols = slice(P * t, P * (t + 1)), slice(n * (t - t0), n * (t - t0 + 1))
+                nc.tensor.matmul_mx(
+                    out=bank_a[:, out_cols], lhsT=w2_c[:, cols].bitcast(FP8X4), lhsT_scale=w2_s[:, cols],
+                    rhs=th_c[c][:].bitcast(FP8X4), rhs_scale=th_s[c][:], start=True, stop=True,
+                )
+            for t in range(t0, t1):
+                cols, out_cols = slice(P * t, P * (t + 1)), slice(n * (t - t0), n * (t - t0 + 1))
+                nc.tensor.matmul_mx(
+                    out=b_of[i][:, out_cols], lhsT=w3_c[:, 2 * P * t : 2 * P * (t + 1)].bitcast(FP4X4),
+                    lhsT_scale=w34_s[:, cols],
+                    rhs=th_c[c][:].bitcast(FP8X4), rhs_scale=th_s[c][:], start=True, stop=True,
+                )
+            if c < last and t1 == PACK:
+                a_of[i] = work.tile([P, BANK], F32, name="a32_%d" % i, tag="th16", align_bytes=64)
             else:
-                a32, h_of[c, t] = stage[2], stage[0]
-            nc.scalar.copy(out=a32[:], in_=bank_a[:])
-            nc.vector.tensor_tensor(out=h_of[c, t][:], in0=bank_b[:], in1=a32[:], op=ALU.min)
+                a_of[i] = work.tile([P, BANK], F32, name="a32_%d" % i, tag="a32", bufs=2)
+            nc.scalar.copy(out=a_of[i][:], in_=bank_a[:])
+            if c < last and t0 == 0:
+                first_product(c + 1)
+                gain_on_scalar(c + 1)
+                weave_th(c + 1)
 
-        def scatter(c, t):
+        def smaller_feature(i):
+            nc.vector.tensor_tensor(out=h32[:], in0=b_of[i][:], in1=a_of[i][:], op=ALU.min)
+
+        def scatter(i):
+            c, t0, t1 = units[i]
             j0, n = S_CHUNKS[c]
-            nc.vector.tensor_tensor(page[t][:].indirect(entries(list2, j0, n)), h_of[c, t][:], wg[c][:, t, :], ALU.mult)
+            for t in range(t0, t1):
+                nc.vector.tensor_tensor(
+                    page[t][:].indirect(entries(list2, j0, n)), h32[:, n * (t - t0) : n * (t - t0 + 1)],
+                    wg[c, t], ALU.mult,
+                )
 
         gelu32 = work.tile([P, PACK, NP], F32, name="gelu32")
         x_g = [None, None]
 
         def review(t, h):
             cols = slice(HALF * h, HALF * (h + 1))
-            nc.vector.tensor_copy(stage[h][:], page[t][:].indirect(entries(list3, HALF * h, HALF)))
-            nc.scalar.activation(out=gelu32[:, t, cols], in_=stage[h][:], func=ACT.Gelu_apprx_tanh, scale=gx_s[:, t : t + 1])
+            nc.vector.tensor_copy(gelu32[:, t, cols], page[t][:].indirect(entries(list3, HALF * h, HALF)))
+            nc.scalar.activation(out=gelu32[:, t, cols], in_=gelu32[:, t, cols], func=ACT.Gelu_apprx_tanh, scale=gx_s[:, t : t + 1])
 
         def review_gain(t, h):
             if x_g[h] is None:
@@ -272,13 +300,13 @@ def tile_list_karaoke_phrase_grading_kernel(
         rest = work.tile([P, PACK, NP], F32, name="rest")
 
         def guide(t, h):
-            nc.vector.tensor_copy(stage[(2, 0, 1, 3)[t]][:], page[t][:].indirect(entries(list4, HALF * h, HALF)))
+            nc.vector.tensor_copy(guide_room[t], page[t][:].indirect(entries(list4, HALF * h, HALF)))
 
         def count_turns(t, h):
             u_of[t, h] = work.tile([P, HALF], F32, name="u%d_%d" % (t, h), tag="u", bufs=4)
             k_of[t, h] = work.tile([P, HALF], U32, name="k%d_%d" % (t, h), tag="k", bufs=4)
             nc.scalar.activation(
-                out=u_of[t, h][:], in_=stage[(2, 0, 1, 3)[t]][:], func=ACT.Copy, scale=turns[:, t : t + 1], bias=0.25
+                out=u_of[t, h][:], in_=guide_room[t], func=ACT.Copy, scale=turns[:, t : t + 1], bias=0.25
             )
             nc.scalar.activation(out=k_of[t, h][:], in_=u_of[t, h][:], func=ACT.Copy, bias=ROUNDER)
 
@@ -295,34 +323,33 @@ def tile_list_karaoke_phrase_grading_kernel(
         gain_on_vector(0)
         quantise_w2(nc.scalar.copy, 0, 2)
         quantise_th(0)
-        smaller_feature(0, 0)
         quantise_w2(nc.scalar.copy, 2, 4)
-
-        for c in range(len(S_CHUNKS)):
-            for t in range(PACK):
-                if (c, t) != (0, 0):
-                    smaller_feature(c, t)
-                scatter(c, t)
-                if c < last and t == 0:
-                    first_product(c + 1)
-                if c < last and t == 1:
-                    gain_on_scalar(c + 1)
-                if c < last and t == 2:
-                    weave_th(c + 1)
-                    quantise_th(c + 1)
-                if c == last:
-                    review(t, 0)
-                    review(t, 1)
-                    review_gain(t, 0)
-                    if t < PACK - 1:
-                        review_gain(t, 1)
-            if c == 1:
+        second_products(0)
+        smaller_feature(0)
+        second_products(1)
+        for i, (c, t0, t1) in enumerate(units):
+            scatter(i)
+            if c < last and t0 == 0:
+                quantise_th(c + 1)
+            if i + 1 < len(units):
+                smaller_feature(i + 1)
+            if c == last:
+                review(t0, 0)
+                review(t0, 1)
+            if i + 2 < len(units):
+                second_products(i + 2)
+            if c == last:
+                review_gain(t0, 0)
+                if t0 < PACK - 1:
+                    review_gain(t0, 1)
+            if (c, t0) == (last, 0):
                 w4_c = work.tile([P, H], I32, name="w4_c", tag="th16", align_bytes=64)
                 nc.vector.tensor_copy(
                     out=w4_c[:].rearrange("p (t q) -> p q t", t=PACK), in_=w4_raw[:].rearrange("p (q t) -> p q t", t=PACK)
                 )
                 nc.scalar.activation(out=turns[:], in_=gg_s[:], func=ACT.Copy, scale=1.0 / (2.0 * math.pi))
 
+        guide_room = [h32[:], wg[last, 3], a_of[len(units) - 1][:], wg[last, 2]]
         x_c = [keep.tile([P, HALF], U32, name="x_c%d" % h, align_bytes=64) for h in range(2)]
         x_s = [keep.tile([P, HALF], U8, name="x_s%d" % h, align_bytes=64) for h in range(2)]
 
@@ -364,20 +391,19 @@ def tile_list_karaoke_phrase_grading_kernel(
             count_turns(t, 0)
         quantise_x(0)
         for t in range(PACK):
-            reduce_turns(t, 0)
             guide(t, 1)
+            reduce_turns(t, 0)
         review_gain(PACK - 1, 1)
         quantise_x(1)
-        modulate(0)
         for t in range(PACK):
             count_turns(t, 1)
             reduce_turns(t, 1)
+        for c in range(len(Y_CHUNKS)):
+            modulate(c)
         planes(0, nc.scalar.copy)
-        modulate(1)
-        modulate(2)
-        planes(1, nc.scalar.copy)
+        planes(1, nc.vector.tensor_copy)
         planes(2, nc.vector.tensor_copy)
         for quad in range(4):
-            nc.sync.dma_start(
+            nc.scalar.dma_start(
                 out=out_2[0, 4 * quad : 4 * quad + 4, :].bitcast(I32), in_=y_s[32 * quad : 32 * quad + 4, :].bitcast(I32)
             )

import math
from contextlib import ExitStack

import concourse.mybir as mybir

F32 = mybir.dt.float32
BF16 = mybir.dt.bfloat16
I32 = mybir.dt.int32
U32 = mybir.dt.uint32
U16 = mybir.dt.uint16
U8 = mybir.dt.uint8
FP8X4 = mybir.dt.float8_e4m3fn_x4
FP4X4 = mybir.dt.float4_e2m1fn_x4
ACT = mybir.ActivationFunctionType
ALU = mybir.AluOpType

P = 128
PACK = 4
K, R, T, S, H, T2, NP = 1024, 512, 2048, 1024, 512, 2048, 1024
FLOPS = 2 * K * R * S + 2 * 2 * R * H * S + 2 * H * H * NP
HALF = 512
BANK = 512
S_CHUNKS = [(0, 256), (256, 256), (512, 512)]
Y_CHUNKS = [(0, 512), (512, 256), (768, 256)]
ROUNDER = 1.5 * 2.0**23


def tile_list_karaoke_phrase_grading_kernel(
    tc, tab_words, tab_scales, offs, offs2, offs3, offs4, w1, gt, w2, w3_words, w3_scales,
    page0, wgs, gx, ge, w4_words, w4_scales, gg, out_0, out_1, out_2,
):
    nc = tc.nc
    with ExitStack() as ctx:
        keep = ctx.enter_context(tc.tile_pool(name="keep", bufs=1))
        work = ctx.enter_context(tc.tile_pool(name="work", bufs=1))
        psum = ctx.enter_context(tc.psum_pool(name="psum", bufs=1))

        def entries(lst, j0, n):
            return lst[:, j0 // 16 : (j0 + n) // 16]

        def weave(ap_tj):
            return ap_tj.rearrange("p t (c i) -> p c t i", i=PACK)

        def woven(ap_jt):
            return ap_jt.rearrange("p (c i t) -> p c t i", i=PACK, t=PACK)

        list1 = keep.tile([P, S // 16], U16, name="list1")
        list2 = keep.tile([P, S // 16], U16, name="list2")
        list3 = keep.tile([P, NP // 16], U16, name="list3")
        list4 = keep.tile([P, NP // 16], U16, name="list4")
        tab_w = [keep.tile([P, T], U32, name="tab_w%d" % a, align_bytes=64) for a in range(2)]
        tab_s = keep.tile([P, T], U8, name="tab_s", align_bytes=64)
        w3_raw = keep.tile([P, 2 * H], U8, name="w3_raw", align_bytes=64)
        w3_c = keep.tile([P, 2 * H], U8, name="w3_c", align_bytes=64)
        w34_raw = keep.tile([P, H], U8, name="w34_raw", align_bytes=64)
        w34_s = keep.tile([P, H], U8, name="w34_s", align_bytes=64)
        w4_raw = keep.tile([P, H], I32, name="w4_raw", align_bytes=64)
        page = [keep.tile([P, T2], F32, name="page%d" % t) for t in range(PACK)]
        gt_s = keep.tile([P, PACK], F32, name="gt_s")
        gx_s = keep.tile([P, PACK], F32, name="gx_s")
        ge_s = keep.tile([P, PACK], F32, name="ge_s")
        gg_s = keep.tile([P, PACK], F32, name="gg_s")
        turns = keep.tile([P, PACK], F32, name="turns")
        warm = keep.tile([P, 1], F32, name="warm")
        warm2 = keep.tile([P, 1], F32, name="warm2")

        nc.gpsimd.memset(w34_raw[:].bitcast(I32), 0)
        nc.gpsimd.memset(tab_s[:].bitcast(I32), 0)
        nc.vector.memset(warm[:], 0.0)
        nc.scalar.activation(out=warm2[:], in_=warm[:], func=ACT.Gelu_apprx_tanh)

        def load_rows(w, a, name):
            raw = work.tile([P, PACK, 512], F32, name=name, tag="raw", bufs=3, align_bytes=64)
            nc.sync.dma_start(out=raw[:], in_=w[512 * a : 512 * (a + 1), :].rearrange("(p j) c -> p j c", j=PACK))
            return raw

        def load_tab(a):
            nc.sync.dma_start(out=tab_w[a][:].bitcast(I32), in_=tab_words[a].rearrange("p n t -> p (n t)").bitcast(I32))

        wg = {}

        def load_wg(c, t0, t1):
            j0, n = S_CHUNKS[c]
            tile = work.tile([P, t1 - t0, n], F32, name="wg%d_%d" % (c, t0), tag="wg%d_%d" % (c, t0), align_bytes=64)
            rows = wgs.rearrange("(q t) j -> q t j", t=PACK)[:, t0:t1, j0 : j0 + n]
            for quad in range(4):
                nc.sync.dma_start(out=tile[32 * quad : 32 * quad + 32, :, :], in_=rows)
            for t in range(t0, t1):
                wg[c, t] = tile[:, t - t0, :]

        def load_page(t):
            nc.sync.dma_start(out=page[t][:], in_=page0.rearrange("(p t) c -> t p c", t=PACK)[t])

        def load_scales(engine, row0, scales):
            for quad in range(4):
                engine.dma_start(
                    out=w34_raw[32 * quad + row0 : 32 * quad + row0 + 4, :].bitcast(I32),
                    in_=scales[0, 4 * quad : 4 * quad + 4, :].bitcast(I32),
                )

        def load_vec(dst, vec):
            nc.sync.dma_start(out=dst[:], in_=vec.rearrange("(p t) -> p t", t=PACK))

        nc.sync.dma_start(list1[:], offs)
        nc.sync.dma_start(out=w3_raw[:].bitcast(I32), in_=w3_words[0].bitcast(I32))
        load_tab(0)
        for quad in range(4):
            nc.sync.dma_start(
                out=tab_s[32 * quad : 32 * quad + 8, :].bitcast(I32),
                in_=tab_scales[:, 4 * quad : 4 * quad + 4, :].bitcast(I32),
            )
        w1_raw = [load_rows(w1, 0, "w1_raw0")]
        load_scales(nc.sync, 0, w3_scales)
        w1_raw.append(load_rows(w1, 1, "w1_raw1"))
        load_tab(1)
        load_scales(nc.sync, 4, w4_scales)
        w2_raw = load_rows(w2, 0, "w2_raw")
        load_vec(gt_s, gt)
        load_vec(gg_s, gg)
        nc.sync.dma_start(list2[:], offs2)
        load_page(0)
        load_wg(0, 0, 2)
        load_page(1)
        load_page(2)
        load_wg(0, 2, 4)
        load_page(3)
        load_wg(1, 0, 2)
        load_wg(1, 2, 4)
        nc.sync.dma_start(list3[:], offs3)
        load_vec(gx_s, gx)
        load_vec(ge_s, ge)
        load_wg(2, 0, 4)
        nc.sync.dma_start(list4[:], offs4)
        nc.sync.dma_start(out=w4_raw[:], in_=w4_words[0].rearrange("p n t -> p (n t)").bitcast(I32))


        nc.vector.tensor_copy(
            out=w3_c[:].rearrange("p (t q b) -> p q t b", t=PACK, b=2),
            in_=w3_raw[:].rearrange("p (q t b) -> p q t b", t=PACK, b=2),
        )

        def round_and_deal(engine_copy, grouped, raw, t0, t1):
            engine_copy(
                out=grouped[:].rearrange("p (t q j) -> p q j t", t=PACK, j=PACK)[:, :, :, t0:t1],
                in_=raw[:].rearrange("p j (q t) -> p q j t", t=PACK)[:, :, :, t0:t1],
            )

        def gather_words(words, a, c):
            j0, n = S_CHUNKS[c]
            v_w[a, c] = words[:, j0 : j0 + n]
            nc.vector.tensor_copy(v_w[a, c], tab_w[a][:].indirect(entries(list1, j0, n)))

        w1_c = [keep.tile([P, R], U32, name="w1_c%d" % a, align_bytes=64) for a in range(2)]
        w1_s = [keep.tile([P, R], U8, name="w1_s%d" % a, align_bytes=64) for a in range(2)]
        w2_c = keep.tile([P, H], U32, name="w2_c", align_bytes=64)
        w2_s = keep.tile([P, H], U8, name="w2_s", align_bytes=64)

        def grouped_tile(name, width):
            return work.tile([P, width], BF16, name=name, tag="grouped", bufs=3, align_bytes=64)

        v_w, v_s = {}, {}

        def gather_scales(c):
            j0, n = S_CHUNKS[c]
            v_s[c] = keep.tile([P, n], U8, name="v_s%d" % c, align_bytes=64)
            nc.vector.tensor_copy(v_s[c][:], tab_s[:].indirect(entries(list1, j0, n)))

        v_w0 = keep.tile([P, S], U32, name="v_w0", align_bytes=64)
        for c in range(len(S_CHUNKS)):
            gather_words(v_w0, 0, c)
            gather_scales(c)
        w1_g0 = grouped_tile("w1_g0", PACK * R)
        round_and_deal(nc.scalar.copy, w1_g0, w1_raw[0], 0, 4)
        w1_g1 = work.tile([P, PACK * R], BF16, name="w1_g1", tag="second_pass", align_bytes=64)
        round_and_deal(nc.scalar.copy, w1_g1, w1_raw[1], 0, 2)
        round_and_deal(nc.vector.tensor_copy, w1_g1, w1_raw[1], 2, 4)
        for a, w1_g in enumerate((w1_g0, w1_g1)):
            nc.vector.quantize_mx(out=w1_c[a][:].bitcast(FP8X4), scales=w1_s[a][:], in_=w1_g[:])
        v_w1 = work.tile([P, S], U32, name="v_w1", tag="second_pass", align_bytes=64)
        for c in range(len(S_CHUNKS)):
            gather_words(v_w1, 1, c)

        th_c, th_s = {}, {}
        th32, th16, th_g = {}, {}, {}

        def first_product(c):
            j0, n = S_CHUNKS[c]
            banks = [psum.tile([P, n], F32, name="z%d_%d" % (c, t), tag="z%d" % t) for t in range(PACK)]
            for a in range(2):
                for t in range(PACK):
                    cols = slice(P * t, P * (t + 1))
                    nc.tensor.matmul_mx(
                        out=banks[t][:],
                        lhsT=w1_c[a][:, cols].bitcast(FP8X4), lhsT_scale=w1_s[a][:, cols],
                        rhs=v_w[a, c].bitcast(FP8X4), rhs_scale=v_s[c][4 * a : P, :],
                        start=(a == 0), stop=(a == 1),
                    )
            th32[c] = work.tile([P, PACK, n], F32, name="th32_%d" % c, tag="th32")
            for t in range(PACK):
                nc.scalar.activation(out=th32[c][:, t, :], in_=banks[t][:], func=ACT.Tanh)

        def gain_on_vector(c):
            j0, n = S_CHUNKS[c]
            th_g[c] = work.tile([P, PACK * n], BF16, name="th_g%d" % c, tag="th_g", bufs=2, align_bytes=64)
            gains = gt_s[:].rearrange("p (c t i) -> p c t i", c=1, i=1).to_broadcast([P, n // PACK, PACK, PACK])
            nc.vector.tensor_tensor(out=woven(th_g[c][:]), in0=weave(th32[c][:]), in1=gains, op=ALU.mult)

        def gain_on_scalar(c):
            j0, n = S_CHUNKS[c]
            th16[c] = work.tile([P, PACK, n], BF16, name="th16_%d" % c, tag="th16", align_bytes=64)
            for t in range(PACK):
                nc.scalar.activation(out=th16[c][:, t, :], in_=th32[c][:, t, :], func=ACT.Copy, scale=gt_s[:, t : t + 1])

        def weave_th(c):
            j0, n = S_CHUNKS[c]
            th_g[c] = work.tile([P, PACK * n], BF16, name="th_g%d" % c, tag="th_g", bufs=2, align_bytes=64)
            nc.scalar.copy(out=woven(th_g[c][:]), in_=weave(th16[c][:]))

        def quantise_th(c):
            j0, n = S_CHUNKS[c]
            place = "wg%d_0" % (c - 1) if c > 0 else "th_c0"
            th_c[c] = work.tile([P, n], U32, name="th_c%d" % c, tag=place, align_bytes=64)
            th_s[c] = keep.tile([P, n], U8, name="th_s%d" % c, align_bytes=64)
            nc.vector.quantize_mx(out=th_c[c][:].bitcast(FP8X4), scales=th_s[c][:], in_=th_g[c][:])

        w2_g = grouped_tile("w2_g", PACK * H)

        def quantise_w2(engine_copy, t0, t1):
            round_and_deal(engine_copy, w2_g, w2_raw, t0, t1)
            cols = slice(P * t0, P * t1)
            nc.vector.quantize_mx(
                out=w2_c[:, cols].bitcast(FP8X4), scales=w2_s[:, cols], in_=w2_g[:, PACK * P * t0 : PACK * P * t1]
            )

        last = len(S_CHUNKS) - 1
        units = []
        for c, (j0, n) in enumerate(S_CHUNKS):
            per_bank = BANK // n
            units.extend((c, t0, t0 + per_bank) for t0 in range(0, PACK, per_bank))
        a_of, b_of = {}, {}
        h32 = keep.tile([P, BANK], F32, name="h32")

        def second_products(i):
            c, t0, t1 = units[i]
            n = S_CHUNKS[c][1]
            bank_a = psum.tile([P, BANK], F32, name="a%d" % i, tag="a", bufs=2)
            b_of[i] = psum.tile([P, BANK], F32, name="b%d" % i, tag="b", bufs=2)
            for t in range(t0, t1):
                cols, out_cols = slice(P * t, P * (t + 1)), slice(n * (t - t0), n * (t - t0 + 1))
                nc.tensor.matmul_mx(
                    out=bank_a[:, out_cols], lhsT=w2_c[:, cols].bitcast(FP8X4), lhsT_scale=w2_s[:, cols],
                    rhs=th_c[c][:].bitcast(FP8X4), rhs_scale=th_s[c][:], start=True, stop=True,
                )
            for t in range(t0, t1):
                cols, out_cols = slice(P * t, P * (t + 1)), slice(n * (t - t0), n * (t - t0 + 1))
                nc.tensor.matmul_mx(
                    out=b_of[i][:, out_cols], lhsT=w3_c[:, 2 * P * t : 2 * P * (t + 1)].bitcast(FP4X4),
                    lhsT_scale=w34_s[:, cols],
                    rhs=th_c[c][:].bitcast(FP8X4), rhs_scale=th_s[c][:], start=True, stop=True,
                )
            if c < last and t1 == PACK:
                a_of[i] = work.tile([P, BANK], F32, name="a32_%d" % i, tag="th16", align_bytes=64)
            else:
                a_of[i] = work.tile([P, BANK], F32, name="a32_%d" % i, tag="a32", bufs=2)
            nc.scalar.copy(out=a_of[i][:], in_=bank_a[:])
            if c < last and t0 == 0:
                first_product(c + 1)
                gain_on_scalar(c + 1)
                weave_th(c + 1)

        def smaller_feature(i):
            nc.vector.tensor_tensor(out=h32[:], in0=b_of[i][:], in1=a_of[i][:], op=ALU.min)

        def scatter(i):
            c, t0, t1 = units[i]
            j0, n = S_CHUNKS[c]
            for t in range(t0, t1):
                nc.vector.tensor_tensor(
                    page[t][:].indirect(entries(list2, j0, n)), h32[:, n * (t - t0) : n * (t - t0 + 1)],
                    wg[c, t], ALU.mult,
                )

        gelu32 = work.tile([P, PACK, NP], F32, name="gelu32")
        x_g = [None, None]

        def review(t, h):
            cols = slice(HALF * h, HALF * (h + 1))
            nc.vector.tensor_copy(gelu32[:, t, cols], page[t][:].indirect(entries(list3, HALF * h, HALF)))
            nc.scalar.activation(out=gelu32[:, t, cols], in_=gelu32[:, t, cols], func=ACT.Gelu_apprx_tanh, scale=gx_s[:, t : t + 1])

        def review_gain(t, h):
            if x_g[h] is None:
                x_g[h] = grouped_tile("x_g%d" % h, PACK * HALF)
            nc.scalar.activation(
                out=x_g[h][:].rearrange("p (j t) -> p t j", t=PACK)[:, t, :], in_=gelu32[:, t, HALF * h : HALF * (h + 1)],
                func=ACT.Copy, scale=ge_s[:, t : t + 1],
            )

        u_of, k_of = {}, {}
        rest = work.tile([P, PACK, NP], F32, name="rest")

        def guide(t, h):
            nc.vector.tensor_copy(guide_room[t], page[t][:].indirect(entries(list4, HALF * h, HALF)))

        def count_turns(t, h):
            u_of[t, h] = work.tile([P, HALF], F32, name="u%d_%d" % (t, h), tag="u", bufs=4)
            k_of[t, h] = work.tile([P, HALF], U32, name="k%d_%d" % (t, h), tag="k", bufs=4)
            nc.scalar.activation(
                out=u_of[t, h][:], in_=guide_room[t], func=ACT.Copy, scale=turns[:, t : t + 1], bias=0.25
            )
            nc.scalar.activation(out=k_of[t, h][:], in_=u_of[t, h][:], func=ACT.Copy, bias=ROUNDER)

        def reduce_turns(t, h):
            nc.vector.scalar_tensor_tensor(
                out=rest[:, t, HALF * h : HALF * (h + 1)], in0=k_of[t, h][:].bitcast(I32), scalar=ROUNDER,
                in1=u_of[t, h][:], op0=ALU.subtract, op1=ALU.subtract,
            )

        first_product(0)
        nc.vector.tensor_copy(
            out=w34_s[:].rearrange("p (t q) -> p q t", t=PACK), in_=w34_raw[:].rearrange("p (q t) -> p q t", t=PACK)
        )
        gain_on_vector(0)
        quantise_w2(nc.scalar.copy, 0, 2)
        quantise_th(0)
        quantise_w2(nc.scalar.copy, 2, 4)
        second_products(0)
        smaller_feature(0)
        second_products(1)
        for i, (c, t0, t1) in enumerate(units):
            scatter(i)
            if c < last and t0 == 0:
                quantise_th(c + 1)
            if i + 1 < len(units):
                smaller_feature(i + 1)
            if c == last:
                review(t0, 0)
                review(t0, 1)
            if i + 2 < len(units):
                second_products(i + 2)
            if c == last:
                review_gain(t0, 0)
                if t0 < PACK - 1:
                    review_gain(t0, 1)
            if (c, t0) == (last, 0):
                w4_c = work.tile([P, H], I32, name="w4_c", tag="th16", align_bytes=64)
                nc.vector.tensor_copy(
                    out=w4_c[:].rearrange("p (t q) -> p q t", t=PACK), in_=w4_raw[:].rearrange("p (q t) -> p q t", t=PACK)
                )
                nc.scalar.activation(out=turns[:], in_=gg_s[:], func=ACT.Copy, scale=1.0 / (2.0 * math.pi))

        guide_room = [h32[:], wg[last, 3], a_of[len(units) - 1][:], wg[last, 2]]
        x_c = [keep.tile([P, HALF], U32, name="x_c%d" % h, align_bytes=64) for h in range(2)]
        x_s = [keep.tile([P, HALF], U8, name="x_s%d" % h, align_bytes=64) for h in range(2)]

        def quantise_x(h):
            nc.vector.quantize_mx(out=x_c[h][:].bitcast(FP8X4), scales=x_s[h][:], in_=x_g[h][:])

        y_s = keep.tile([P, NP], U8, name="y_s", align_bytes=64)
        out_rows = out_0.rearrange("(p t) j -> p t j", t=PACK)
        out_words = out_1[0].rearrange("p n t -> p (n t)").bitcast(I32)
        cos32 = gelu32
        y32 = {}

        def modulate(c):
            j0, n = Y_CHUNKS[c]
            h, cols, xc = j0 // HALF, slice(j0, j0 + n), slice(j0 % HALF, j0 % HALF + n)
            y32[c] = work.tile([P, PACK, n], F32, name="y32_%d" % c, tag="raw", bufs=3, align_bytes=64)
            for t in range(PACK):
                wc = slice(P * t, P * (t + 1))
                bank = psum.tile([P, n], F32, name="f%d_%d" % (c, t), tag="z%d" % t)
                nc.tensor.matmul_mx(
                    out=bank[:], lhsT=w4_c[:, wc].bitcast(FP8X4), lhsT_scale=w34_s[4:P, wc],
                    rhs=x_c[h][:, xc].bitcast(FP8X4), rhs_scale=x_s[h][:, xc], start=True, stop=True,
                )
                nc.scalar.activation(out=cos32[:, t, cols], in_=rest[:, t, cols], func=ACT.Sin, scale=-2.0 * math.pi)
                nc.vector.tensor_tensor(out=y32[c][:, t, :], in0=bank[:], in1=cos32[:, t, cols], op=ALU.mult)
            nc.sync.dma_start(out=out_rows[:, :, cols], in_=y32[c][:])

        def planes(c, engine_copy):
            j0, n = Y_CHUNKS[c]
            cols = slice(j0, j0 + n)
            y_g = grouped_tile("y_g%d" % c, PACK * n)
            engine_copy(out=woven(y_g[:]), in_=weave(y32[c][:]))
            y_c = keep.tile([P, n], U32, name="y_c%d" % c, align_bytes=64)
            nc.vector.quantize_mx(out=y_c[:].bitcast(FP8X4), scales=y_s[:, cols], in_=y_g[:])
            nc.sync.dma_start(out=out_words[:, cols], in_=y_c[:].bitcast(I32))

        for t in range(PACK):
            guide(t, 0)
            count_turns(t, 0)
        quantise_x(0)
        for t in range(PACK):
            guide(t, 1)
            reduce_turns(t, 0)
        review_gain(PACK - 1, 1)
        quantise_x(1)
        for t in range(PACK):
            count_turns(t, 1)
            reduce_turns(t, 1)
        for c in range(len(Y_CHUNKS)):
            modulate(c)
        planes(0, nc.scalar.copy)
        planes(1, nc.vector.tensor_copy)
        planes(2, nc.vector.tensor_copy)
        for quad in range(4):
            nc.scalar.dma_start(
                out=out_2[0, 4 * quad : 4 * quad + 4, :].bitcast(I32), in_=y_s[32 * quad : 32 * quad + 4, :].bitcast(I32)
            )
